import numpy as np
CORES = [127,119,111,103,95,87,79,71,63,55,47,39,31,23,15,7]
N = 16
ROOT = 0
WIDTHS = [256,51,512,0,512,0,0,512,256,256,512,0,512,51,512,256]
OFF = [0,256,307,819,819,1331,1331,1331,1843,2099,2355,2867,2867,3379,3430,3942]
C = 4198
def setup_inputs(rng):
    return {"x": rng.standard_normal((N, 128, C), dtype=np.float32)}
def reference(x):
    YW = max(WIDTHS)
    y = np.full((N, 128, YW), np.nan, x.dtype)
    for r in range(N):
        y[r][:, :WIDTHS[r]] = x[ROOT][:, OFF[r]:OFF[r] + WIDTHS[r]]
    return {"y": y}

@@ -1,0 +1,93 @@
+from concourse.bass import DstId, RemoteDMATransfer
+
+E03, E47, E07 = 0x000F, 0x00F0, 0x00FF
+E8B, ECF, E8F = 0x0F00, 0xF000, 0xFF00
+
+WIDTHS = [256, 51, 512, 0, 512, 0, 0, 512, 256, 256, 512, 0, 512, 51, 512, 256]
+NCH = [2 if w == 512 else 1 for w in WIDTHS]
+
+CALLS = [
+    [(12, 0, [120], E8B), (7, 0, [122], ECF), (2, 0, [], E03), (14, 0, [6], E47)],
+    [(12, 1, [121], E8B), (7, 1, [123], ECF), (2, 1, [], E03), (14, 1, [6], E47)],
+    [(10, 0, [120], E8B), (10, 1, [121], ECF), (4, 0, [], E03), (9, 0, [], E47)],
+    [(4, 1, [], E03), (15, 0, [], E47)],
+    [(8, 0, [], E07)],
+    [(1, 0, [], E03), (13, 0, [], E47)],
+]
+LOAD_ORDER = [12, 7, 2, 14, 10, 4, 9, 15, 8, 1, 13]
+
+SCRATCH = {}
+SEMAPHORES = ["sent", "own", "go", "st0", "st1"]
+for rr in range(1, 16):
+    if WIDTHS[rr]:
+        SCRATCH["p%d" % rr] = ("dram", [NCH[rr], 128, WIDTHS[rr] // NCH[rr]], "float32")
+        SEMAPHORES.append("l%d" % rr)
+        for kk in range(NCH[rr]):
+            SEMAPHORES.append("a%d_%d" % (rr, kk))
+
+
+def pop(m):
+    return bin(m).count("1")
+
+
+def rank_program(g, core, T, topo):
+    W = T.tables["WIDTHS"]
+    OFF = T.tables["OFF"]
+    root = T.cores[0]
+
+    def transfer(r, k, dst, m):
+        rid, pid, se = topo.addr(dst)
+        return RemoteDMATransfer(dst_ids=[DstId(rid=rid, pnc=pid)], dma_engine_mask=m,
+                                 remote_sem=T.sem["a%d_%d" % (r, k)],
+                                 src=T["p%d" % r][k], dst=T["p%d" % r][k])
+
+    if core == root:
+        qs = [g.sync, g.scalar]
+        for i, r in enumerate(LOAD_ORDER):
+            out = T["p%d" % r][:] if NCH[r] > 1 else T["p%d" % r][0]
+            qs[i % 2].dma_start(out, T.x[:, OFF[r]:OFF[r] + W[r]]).then_inc(T.sem["l%d" % r], 16)
+        g.scalar.wait_ge(T.sem.go, 1)
+        g.scalar.dma_start(T.y[:, 0:W[0]], T.x[:, OFF[0]:OFF[0] + W[0]]).then_inc(T.sem.own, 16)
+        g.scalar.wait_ge(T.sem.own, 16)
+        waited = set()
+        total = 0
+        for call in CALLS:
+            trs = []
+            for (r, k, via, m) in call:
+                if r not in waited:
+                    g.wait_ge(T.sem["l%d" % r], 16)
+                    waited.add(r)
+                trs.append(transfer(r, k, (via + [T.cores[r]])[0], m))
+                total += pop(m)
+            g.remote_dma_fused(trs, local_sem=T.sem.sent)
+        g.sem_inc(T.sem.go, 1)
+        g.wait_ge(T.sem.sent, total)
+        return
+
+    total = 0
+    for call in CALLS:
+        for (r, k, via, m) in call:
+            hops = [root] + via + [T.cores[r]]
+            for i in range(1, len(hops) - 1):
+                if hops[i] == core:
+                    g.wait_ge(T.sem["a%d_%d" % (r, k)], pop(m if i == 1 else E07))
+                    rid, pid, se = topo.addr(hops[i + 1])
+                    g.remote_dma(T["p%d" % r][k], T["p%d" % r][k], T.sem["a%d_%d" % (r, k)], T.sem.sent,
+                                 pid, rid, E07)
+                    total += pop(E07)
+    if total:
+        g.wait_ge(T.sem.sent, total)
+
+    rank = T.rank_of(core)
+    if rank is None or W[rank] == 0:
+        return
+    for call in CALLS:
+        for (r, k, via, m) in call:
+            if r != rank:
+                continue
+            q = g.sync if k == 0 else g.scalar
+            st = T.sem["st%d" % k]
+            rows = 128 // NCH[r]
+            q.wait_ge(T.sem["a%d_%d" % (r, k)], pop(E07 if via else m))
+            q.dma_start(T.y[k * rows:(k + 1) * rows, 0:W[r]], T["p%d" % r][k]).then_inc(st, 16)
+            q.wait_ge(st, 16)

@@ -9,20 +9,21 @@ NCH = [2 if w == 512 else 1 for w in WIDTHS]
 CALLS = [
     [(12, 0, [120], E8B), (7, 0, [122], ECF), (2, 0, [], E03), (14, 0, [6], E47)],
     [(12, 1, [121], E8B), (7, 1, [123], ECF), (2, 1, [], E03), (14, 1, [6], E47)],
-    [(10, 0, [120], E8B), (10, 1, [121], ECF), (4, 0, [], E03), (9, 0, [], E47)],
+    [(10, 0, [120], E8B), (10, 1, [121], ECF)],
+    [(8, 0, [124], E8F)],
+    [(4, 0, [], E03), (9, 0, [], E47)],
     [(4, 1, [], E03), (15, 0, [], E47)],
-    [(8, 0, [], E07)],
-    [(1, 0, [], E03), (13, 0, [], E47)],
+    [(1, 0, [123], E8B), (13, 0, [122], ECF)],
 ]
-LOAD_ORDER = [12, 7, 2, 14, 10, 4, 9, 15, 8, 1, 13]
+GATES = [None, None, None, None, 0, None, None]
 
 SCRATCH = {}
-SEMAPHORES = ["sent", "own", "go", "st0", "st1"]
+SEMAPHORES = ["sent", "own", "go", "st0", "st1", "st2", "st3"] + ["g%d" % j for j in range(len(CALLS))]
 for rr in range(1, 16):
     if WIDTHS[rr]:
         SCRATCH["p%d" % rr] = ("dram", [NCH[rr], 128, WIDTHS[rr] // NCH[rr]], "float32")
-        SEMAPHORES.append("l%d" % rr)
         for kk in range(NCH[rr]):
+            SEMAPHORES.append("l%d_%d" % (rr, kk))
             SEMAPHORES.append("a%d_%d" % (rr, kk))
 
 
@@ -43,23 +44,32 @@ def rank_program(g, core, T, topo):
 
     if core == root:
         qs = [g.sync, g.scalar]
-        for i, r in enumerate(LOAD_ORDER):
-            out = T["p%d" % r][:] if NCH[r] > 1 else T["p%d" % r][0]
-            qs[i % 2].dma_start(out, T.x[:, OFF[r]:OFF[r] + W[r]]).then_inc(T.sem["l%d" % r], 16)
+        i = 0
+        gated = set()
+        for j, call in enumerate(CALLS):
+            if GATES[j] is not None:
+                for q in qs:
+                    q.wait_ge(T.sem["g%d" % GATES[j]], 1)
+                gated.add(GATES[j])
+            for (r, k, via, m) in call:
+                q = qs[i % 2]
+                rows = 128 // NCH[r]
+                q.dma_start(T["p%d" % r][k], T.x[k * rows:(k + 1) * rows, OFF[r]:OFF[r] + W[r]]).then_inc(
+                    T.sem["l%d_%d" % (r, k)], 16)
+                i += 1
         g.scalar.wait_ge(T.sem.go, 1)
         g.scalar.dma_start(T.y[:, 0:W[0]], T.x[:, OFF[0]:OFF[0] + W[0]]).then_inc(T.sem.own, 16)
         g.scalar.wait_ge(T.sem.own, 16)
-        waited = set()
         total = 0
-        for call in CALLS:
+        for j, call in enumerate(CALLS):
             trs = []
             for (r, k, via, m) in call:
-                if r not in waited:
-                    g.wait_ge(T.sem["l%d" % r], 16)
-                    waited.add(r)
+                g.wait_ge(T.sem["l%d_%d" % (r, k)], 16)
                 trs.append(transfer(r, k, (via + [T.cores[r]])[0], m))
                 total += pop(m)
             g.remote_dma_fused(trs, local_sem=T.sem.sent)
+            if j in gated:
+                g.sem_inc(T.sem["g%d" % j], 1)
         g.sem_inc(T.sem.go, 1)
         g.wait_ge(T.sem.sent, total)
         return
@@ -85,9 +95,11 @@ def rank_program(g, core, T, topo):
         for (r, k, via, m) in call:
             if r != rank:
                 continue
-            q = g.sync if k == 0 else g.scalar
+            q = g.sync if k % 2 == 0 else g.scalar
             st = T.sem["st%d" % k]
             rows = 128 // NCH[r]
             q.wait_ge(T.sem["a%d_%d" % (r, k)], pop(E07 if via else m))
             q.dma_start(T.y[k * rows:(k + 1) * rows, 0:W[r]], T["p%d" % r][k]).then_inc(st, 16)
-            q.wait_ge(st, 16)
+    for k in range(NCH[rank]):
+        q = g.sync if k % 2 == 0 else g.scalar
+        q.wait_ge(T.sem["st%d" % k], 16)

from concourse.bass import DstId, RemoteDMATransfer

E03, E47, E07 = 0x000F, 0x00F0, 0x00FF
E8B, ECF, E8F = 0x0F00, 0xF000, 0xFF00

WIDTHS = [256, 51, 512, 0, 512, 0, 0, 512, 256, 256, 512, 0, 512, 51, 512, 256]
NCH = [2 if w == 512 else 1 for w in WIDTHS]

CALLS = [
    [(12, 0, [120], E8B), (7, 0, [122], ECF), (2, 0, [], E03), (14, 0, [6], E47)],
    [(12, 1, [121], E8B), (7, 1, [123], ECF), (2, 1, [], E03), (14, 1, [6], E47)],
    [(10, 0, [120], E8B), (10, 1, [121], ECF)],
    [(8, 0, [124], E8F)],
    [(4, 0, [], E03), (9, 0, [], E47)],
    [(4, 1, [], E03), (15, 0, [], E47)],
    [(1, 0, [123], E8B), (13, 0, [122], ECF)],
]
GATES = [None, None, None, None, 0, None, None]

SCRATCH = {}
SEMAPHORES = ["sent", "own", "go", "st0", "st1", "st2", "st3"] + ["g%d" % j for j in range(len(CALLS))]
for rr in range(1, 16):
    if WIDTHS[rr]:
        SCRATCH["p%d" % rr] = ("dram", [NCH[rr], 128, WIDTHS[rr] // NCH[rr]], "float32")
        for kk in range(NCH[rr]):
            SEMAPHORES.append("l%d_%d" % (rr, kk))
            SEMAPHORES.append("a%d_%d" % (rr, kk))


def pop(m):
    return bin(m).count("1")


def rank_program(g, core, T, topo):
    W = T.tables["WIDTHS"]
    OFF = T.tables["OFF"]
    root = T.cores[0]

    def transfer(r, k, dst, m):
        rid, pid, se = topo.addr(dst)
        return RemoteDMATransfer(dst_ids=[DstId(rid=rid, pnc=pid)], dma_engine_mask=m,
                                 remote_sem=T.sem["a%d_%d" % (r, k)],
                                 src=T["p%d" % r][k], dst=T["p%d" % r][k])

    if core == root:
        qs = [g.sync, g.scalar]
        i = 0
        gated = set()
        for j, call in enumerate(CALLS):
            if GATES[j] is not None:
                for q in qs:
                    q.wait_ge(T.sem["g%d" % GATES[j]], 1)
                gated.add(GATES[j])
            for (r, k, via, m) in call:
                q = qs[i % 2]
                rows = 128 // NCH[r]
                q.dma_start(T["p%d" % r][k], T.x[k * rows:(k + 1) * rows, OFF[r]:OFF[r] + W[r]]).then_inc(
                    T.sem["l%d_%d" % (r, k)], 16)
                i += 1
        g.scalar.wait_ge(T.sem.go, 1)
        g.scalar.dma_start(T.y[:, 0:W[0]], T.x[:, OFF[0]:OFF[0] + W[0]]).then_inc(T.sem.own, 16)
        g.scalar.wait_ge(T.sem.own, 16)
        total = 0
        for j, call in enumerate(CALLS):
            trs = []
            for (r, k, via, m) in call:
                g.wait_ge(T.sem["l%d_%d" % (r, k)], 16)
                trs.append(transfer(r, k, (via + [T.cores[r]])[0], m))
                total += pop(m)
            g.remote_dma_fused(trs, local_sem=T.sem.sent)
            if j in gated:
                g.sem_inc(T.sem["g%d" % j], 1)
        g.sem_inc(T.sem.go, 1)
        g.wait_ge(T.sem.sent, total)
        return

    total = 0
    for call in CALLS:
        for (r, k, via, m) in call:
            hops = [root] + via + [T.cores[r]]
            for i in range(1, len(hops) - 1):
                if hops[i] == core:
                    g.wait_ge(T.sem["a%d_%d" % (r, k)], pop(m if i == 1 else E07))
                    rid, pid, se = topo.addr(hops[i + 1])
                    g.remote_dma(T["p%d" % r][k], T["p%d" % r][k], T.sem["a%d_%d" % (r, k)], T.sem.sent,
                                 pid, rid, E07)
                    total += pop(E07)
    if total:
        g.wait_ge(T.sem.sent, total)

    rank = T.rank_of(core)
    if rank is None or W[rank] == 0:
        return
    for call in CALLS:
        for (r, k, via, m) in call:
            if r != rank:
                continue
            q = g.sync if k % 2 == 0 else g.scalar
            st = T.sem["st%d" % k]
            rows = 128 // NCH[r]
            q.wait_ge(T.sem["a%d_%d" % (r, k)], pop(E07 if via else m))
            q.dma_start(T.y[k * rows:(k + 1) * rows, 0:W[r]], T["p%d" % r][k]).then_inc(st, 16)
    for k in range(NCH[rank]):
        q = g.sync if k % 2 == 0 else g.scalar
        q.wait_ge(T.sem["st%d" % k], 16)
